import numpy as np
import ml_dtypes


def mxq(x, axis, fmt="e4m3"):
    dtype, down = {"e4m3": (ml_dtypes.float8_e4m3fn, 7), "e5m2": (ml_dtypes.float8_e5m2, 14)}[fmt]
    v = np.moveaxis(np.asarray(x, np.float32).astype(ml_dtypes.bfloat16).astype(np.float64), axis, -1)
    blocks = v.reshape(v.shape[:-1] + (-1, 32))
    amax = np.abs(blocks).max(-1, keepdims=True)
    byte = np.maximum(np.where(amax > 0, np.frexp(amax)[1] - 1 + 127, 0) - down, 1)
    scale = np.exp2(byte - 127.0)
    codes = (blocks / scale).astype(np.float32).astype(dtype).astype(np.float64)
    return np.moveaxis((codes * scale).reshape(v.shape), -1, axis)


WIDE = False


def mx_kscale(k):
    if not WIDE:
        return np.ones(k)
    levels = np.array([10, -10, 5, -5, 0])
    if k % 512:
        return np.exp2(np.random.permutation(np.resize(levels, k // 32))).repeat(32)
    a = np.empty((k // 512, 16))
    for p in range(k // 512):
        a[p, :8] = np.random.permutation(np.resize(levels, 8))
        for g in range(8):
            far = levels[np.abs(levels - a[p, g]) >= 10]
            a[p, g + 8] = far[np.random.randint(len(far))]
    return np.exp2(a.ravel()).repeat(32)


def f64(x):
    return np.asarray(x).astype(np.float64)


def striped(idx):
    return np.tile(idx.reshape(-1, 16).T, (8, 1)).astype(np.uint16)


def unstriped(offs):
    return offs[:16].T.reshape(-1).astype(np.int64)


E2M1 = np.array([0.0, 0.5, 1.0, 1.5, 2.0, 3.0, 4.0, 6.0, -0.0, -0.5, -1.0, -1.5, -2.0, -3.0, -4.0, -6.0])


def pack_weight(w, fmt):
    k, n = w.shape
    w = f64(np.asarray(w, np.float32).astype(ml_dtypes.bfloat16)).reshape(k // 32, 32, n)
    amax = np.abs(w).max(1)
    if fmt == "e4m3":
        byte = np.frexp(amax)[1] - 1 + 127 - 7
    else:
        mant, ex = np.frexp(amax / 6.0)
        byte = np.where(mant > 0.5, ex, ex - 1) + 127
    byte = np.clip(np.where(amax > 0, byte, 1), 1, 254)
    scaled = (w * np.exp2(127.0 - byte)[:, None, :]).reshape(k, n).astype(np.float32)
    by_word = np.ascontiguousarray(scaled.reshape(k // 512, 128, 4, n).transpose(0, 1, 3, 2))
    if fmt == "e4m3":
        words = by_word.astype(ml_dtypes.float8_e4m3fn).view(np.uint8)
    else:
        c = by_word.astype(ml_dtypes.float4_e2m1fn).view(np.uint8) & 0xF
        words = (c[..., 0::2] | (c[..., 1::2] << 4)).reshape(k // 512, 128, 2 * n)
    return np.ascontiguousarray(words), np.ascontiguousarray(byte.astype(np.uint8).reshape(k // 512, 16, n))


def unpack_weight(words, scales, fmt):
    g, _, n = scales.shape
    words = np.ascontiguousarray(words).reshape(g, 128, n, -1)
    if fmt == "e4m3":
        vals = words.view(ml_dtypes.float8_e4m3fn).astype(np.float64)
    else:
        nib = np.empty((g, 128, n, 4), np.uint8)
        nib[..., 0::2] = words & 0xF
        nib[..., 1::2] = words >> 4
        vals = E2M1[nib]
    vals = vals * np.repeat(np.exp2(scales.astype(np.float64) - 127.0), 8, axis=1)[..., None]
    return vals.transpose(0, 1, 3, 2).reshape(g * 512, n)


def gelu(v):
    return 0.5 * v * (1.0 + np.tanh(np.sqrt(2.0 / np.pi) * (v + 0.044715 * v**3)))


def striped8(idx):
    return np.concatenate([v.reshape(-1, 16).T for v in idx]).astype(np.uint16)


def unstriped8(offs):
    return np.stack([offs[16 * g:16 * g + 16].T.reshape(-1) for g in range(8)]).astype(np.int64)


def runs(v, idx8):
    k = np.arange(v.shape[0])
    return v[k[:, None], idx8[k % 512 // 64]]


def often(T, S):
    return np.random.permutation(T)[(T * np.random.uniform(0, 1, S) ** 4).astype(np.int64)]


K, T, S, P, H, N, L = 512, 2048, 1024, 512, 1024, 768, 8


def setup_inputs():
    n = np.random.standard_normal
    s = mx_kscale(K)[:, None]
    u = mx_kscale(H)[:, None]
    d = {}
    mark = np.sign(n(K))[:, None]
    level = np.random.uniform(-1.8, 1.8, T)[None, :]
    d["tab_words"], d["tab_scales"] = pack_weight((mark * level + 0.5 * n((K, T))) * s, "e4m3")
    d["offs"] = striped8(np.stack([often(T, S) for _ in range(L)]))
    own = (np.arange(K) * L // K)[:, None] == (np.arange(H) % L)[None, :]
    w1 = 0.17 * n((K, H)) / K**0.5 + mark * np.sign(n(H))[None, :] * own * L / K
    d["w1"] = (w1 / s).astype(np.float32)
    d["pos1"] = striped(np.random.permutation(S)[:P])
    d["pos2"] = striped(np.random.permutation(S)[:P])
    d["lift"] = (np.exp(0.3 * n(H)) * u[:, 0]).astype(np.float32)
    d["w4_words"], d["w4_scales"] = pack_weight(2.0 * n((H, N)) / H**0.5 / u, "e2m1")
    d["base"] = (0.5 * n((N, P))).astype(np.float32)
    return d


def reference(tab_words, tab_scales, offs, w1, pos1, pos2, lift, w4_words, w4_scales, base):
    v = runs(unpack_weight(tab_words, tab_scales, "e4m3"), unstriped8(offs))
    a = mxq(f64(w1), 0, "e4m3").T @ v
    h = a + np.cos(a)
    this_year = h[:, unstriped(pos1)]
    last_year = h[:, unstriped(pos2)]
    change = 1.0 / (1.0 + np.exp(-(this_year - last_year)))
    z = change * last_year * f64(lift)[:, None]
    w4 = unpack_weight(w4_words, w4_scales, "e2m1")
    y = w4.T @ mxq(z, 0, "e4m3")
    return y + f64(base)

@@ -1,0 +1,251 @@
+import math
+from contextlib import ExitStack
+
+import concourse.mybir as mybir
+
+K, T, S, PAIRS, H, N = 512, 2048, 1024, 512, 1024, 768
+FLOPS = 2 * K * H * S + 2 * H * N * PAIRS
+
+F32 = mybir.dt.float32
+BF16 = mybir.dt.bfloat16
+I32 = mybir.dt.int32
+U32 = mybir.dt.uint32
+U16 = mybir.dt.uint16
+U8 = mybir.dt.uint8
+FP8X4 = mybir.dt.float8_e4m3fn_x4
+FP4X4 = mybir.dt.float4_e2m1fn_x4
+ACT = mybir.ActivationFunctionType
+ALU = mybir.AluOpType
+
+P = 128
+PACK = 4
+K_PASS = P * PACK
+BANK = 512
+QUADRANT = 32
+STRADDLE = 14
+PASSES = H // K_PASS
+SLICES = H // P
+N_TILES = N // P
+HALF = PAIRS // 2
+MM = 128
+
+
+def tile_list_audit_schedule_priorities_kernel(
+    tc, tab_words, tab_scales, offs, w1, pos1, pos2, lift, w4_words, w4_scales, base, out
+):
+    nc = tc.nc
+    with ExitStack() as ctx:
+        keep = ctx.enter_context(tc.tile_pool(name="keep", bufs=1))
+        ring = ctx.enter_context(tc.tile_pool(name="ring", bufs=3))
+        psum = ctx.enter_context(tc.psum_pool(name="psum", bufs=8))
+
+        offs_t = keep.tile([P, S // 16], U16, name="offs_t")
+        pos1_t = keep.tile([P, PAIRS // 16], U16, name="pos1_t")
+        pos2_t = keep.tile([P, PAIRS // 16], U16, name="pos2_t")
+        tab_w = keep.tile([P, T], I32, name="tab_w", align_bytes=64)
+        tab_s = keep.tile([P, T], U8, name="tab_s", align_bytes=64)
+        v_w = [keep.tile([P, BANK], U32, name="v_w%d" % i, align_bytes=64) for i in range(2)]
+        v_s_picked = keep.tile([P, S], U8, name="v_s_picked", align_bytes=64)
+        v_s = keep.tile([P, S], U8, name="v_s", align_bytes=64)
+        w4_w = keep.tile([P, PASSES, 2 * N], U8, name="w4_w", align_bytes=64)
+        w4_s = keep.tile([P, PASSES, N], U8, name="w4_s", align_bytes=64)
+        zero = keep.tile([P, 1], F32, name="zero")
+        no_bias = keep.tile([P, 1], F32, name="no_bias")
+        lift_t = keep.tile([P, PASSES, PACK], F32, name="lift_t")
+        half_lift = keep.tile([P, PASSES * PACK], F32, name="half_lift")
+        base_t = keep.tile([P, N_TILES, PAIRS], F32, name="base_t")
+
+        nc.vector.memset(tab_s[:].bitcast(I32), 0)
+        nc.gpsimd.memset(zero[:], 0.0)
+        nc.gpsimd.memset(v_s[:].bitcast(I32), 0)
+        nc.gpsimd.memset(w4_s[:].rearrange("p a c -> p (a c)").bitcast(I32), 0)
+        nc.scalar.activation(no_bias[:], zero[:], ACT.Silu)
+
+        nc.sync.dma_start(offs_t[:], offs)
+        for d in range(4):
+            r0 = QUADRANT * d + STRADDLE
+            nc.sync.dma_start(tab_s[r0 : r0 + 4, :].bitcast(I32), tab_scales[0, 4 * d : 4 * d + 4, :].bitcast(I32))
+        w1_rows = w1.rearrange("(p j) c -> p j c", j=PACK)
+        w1_first = [keep.tile([P, PACK, K_PASS // 2], F32, name="w1_first%d" % i) for i in range(2)]
+        nc.sync.dma_start(w1_first[0][:], w1_rows[:, :, 0:256])
+        nc.sync.dma_start(tab_w[:], tab_words[0].rearrange("p t i -> p (t i)").bitcast(I32))
+        nc.sync.dma_start(w1_first[1][:], w1_rows[:, :, 256:512])
+
+        nc.vector.tensor_copy(v_s_picked[:], tab_s[:].indirect(offs_t[:]))
+        for d in range(4):
+            r0 = QUADRANT * d
+            nc.sync.dma_start(
+                v_s[r0 : r0 + 4, :].bitcast(I32), v_s_picked[r0 + STRADDLE : r0 + STRADDLE + 4, :].bitcast(I32)
+            )
+
+        w1_second = keep.tile([P, PACK, K_PASS], F32, name="w1_second")
+        nc.sync.dma_start(w1_second[:], w1_rows[:, :, K_PASS:])
+        nc.sync.dma_start(pos2_t[:], pos2)
+        nc.sync.dma_start(pos1_t[:], pos1)
+        nc.sync.dma_start(lift_t[:], lift.rearrange("(a p t) -> p a t", p=P, t=PACK))
+        nc.sync.dma_start(w4_w[:].bitcast(I32), w4_words.rearrange("a p c -> p a c").bitcast(I32))
+        for d in range(4):
+            r0 = QUADRANT * d
+            nc.sync.dma_start(
+                w4_s[r0 : r0 + 4, :, :].bitcast(I32),
+                w4_scales[:, 4 * d : 4 * d + 4, :].rearrange("a q c -> q a c").bitcast(I32),
+            )
+        nc.sync.dma_start(base_t[:], base.rearrange("(nt p) m -> p nt m", p=P))
+        nc.gpsimd.tensor_scalar(half_lift[:], lift_t[:].rearrange("p a t -> p (a t)"), 0.5, 0.0, ALU.mult, ALU.add)
+
+        w1_b = [keep.tile([P, PACK, P, PACK], BF16, name="w1_b%d" % a, align_bytes=64) for a in range(PASSES)]
+        w1_w = [keep.tile([P, K_PASS], U32, name="w1_w%d" % a, align_bytes=64) for a in range(PASSES)]
+        w1_s = [keep.tile([P, K_PASS], U8, name="w1_s%d" % a, align_bytes=64) for a in range(PASSES)]
+
+        def quantise_w1(a, t0, t1):
+            cols = slice(P * t0, P * t1)
+            nc.vector.quantize_mx(
+                out=w1_w[a][:, cols].bitcast(FP8X4), scales=w1_s[a][:, cols],
+                in_=w1_b[a][:, t0:t1, :, :].rearrange("p t m j -> p (t m j)"),
+            )
+
+        for i in range(2):
+            nc.scalar.copy(
+                w1_b[0][:, :, 64 * i : 64 * (i + 1), :].rearrange("p t m j -> p m j t"),
+                w1_first[i][:].rearrange("p j (m t) -> p m j t", t=PACK),
+            )
+        for i in range(2):
+            nc.vector.tensor_copy(v_w[i][:], tab_w[:].bitcast(U32).indirect(offs_t[:, 32 * i : 32 * (i + 1)]))
+        quantise_w1(0, 0, 2)
+        quantise_w1(0, 2, 4)
+        nc.vector.tensor_copy(
+            w1_b[1][:].rearrange("p t m j -> p m j t"), w1_second[:].rearrange("p j (m t) -> p m j t", t=PACK)
+        )
+        quantise_w1(1, 0, 4)
+
+        last = [keep.tile([P, PACK, PAIRS], F32, name="last%d" % a) for a in range(PASSES)]
+        gate = [keep.tile([P, PACK, PAIRS], F32, name="gate%d" % a) for a in range(PASSES)]
+        first_sines = keep.tile([P, 2, BANK], F32, name="first_sines")
+        z_b = {}
+        z_w = [keep.tile([P, PAIRS], U32, name="z_w%d" % a, align_bytes=64) for a in range(PASSES)]
+        z_s = [keep.tile([P, PAIRS], U8, name="z_s%d" % a, align_bytes=64) for a in range(PASSES)]
+        a_banks, squares, h_tiles = {}, {}, {}
+
+        def sine_slot(s, i):
+            if s <= 1:
+                return first_sines[:, i, :]
+            a, t = divmod(s - 1, PACK)
+            return (last, gate)[i][a][:, t, :]
+
+        def first_stage(s):
+            a, t = divmod(s, PACK)
+            cols = slice(P * t, P * (t + 1))
+            for i in range(2):
+                bank = psum.tile([P, BANK], F32, name="bank")
+                a_banks[s, i] = bank
+                nc.tensor.matmul_mx(
+                    out=bank[:], lhsT=w1_w[a][:, cols].bitcast(FP8X4), lhsT_scale=w1_s[a][:, cols],
+                    rhs=v_w[i][:].bitcast(FP8X4), rhs_scale=v_s[:, BANK * i : BANK * (i + 1)], start=True, stop=True,
+                )
+            for i in range(2):
+                nc.scalar.activation(sine_slot(s, i), a_banks[s, i][:], ACT.Sin, bias=no_bias[:], scale=0.5)
+            for i in range(2):
+                if (s, i) == (SLICES - 1, 1):
+                    squares[s, i] = keep.tile([P, BANK], F32, name="late", align_bytes=64)
+                else:
+                    squares[s, i] = ring.tile([P, BANK], F32, name="square", bufs=4)
+                nc.scalar.activation(squares[s, i][:], sine_slot(s, i), ACT.Square, scale=math.sqrt(2.0))
+            h_tiles[s] = ring.tile([P, S], F32, name="h")
+
+        def features(s, i):
+            nc.vector.scalar_tensor_tensor(
+                h_tiles[s][:, BANK * i : BANK * (i + 1)], a_banks[s, i][:], 1.0, squares[s, i][:], ALU.add, ALU.subtract
+            )
+
+        def pick_last(s):
+            a, t = divmod(s, PACK)
+            nc.vector.tensor_copy(last[a][:, t, :], h_tiles[s][:].indirect(pos2_t[:]))
+
+        def pick_change(s):
+            a, t = divmod(s, PACK)
+            nc.vector.tensor_tensor(gate[a][:, t, :], h_tiles[s][:].indirect(pos1_t[:]), last[a][:, t, :], ALU.subtract)
+
+        def make_gate(s, cols):
+            a, t = divmod(s, PACK)
+            g = gate[a][:, t, cols]
+            nc.scalar.activation(g, g, ACT.Tanh, scale=0.5)
+            nc.scalar.activation(g, g, ACT.Identity, bias=half_lift[:, s : s + 1], scale=half_lift[:, s : s + 1])
+
+        halves = [slice(HALF * i, HALF * (i + 1)) for i in range(2)]
+
+        def product(a, i):
+            cols = halves[i]
+            nc.vector.tensor_tensor(
+                z_b[a][:, PACK * cols.start : PACK * cols.stop].rearrange("p (c i t) -> p c t i", i=4, t=PACK),
+                gate[a][:, :, cols].rearrange("p t (c i) -> p c t i", i=4),
+                last[a][:, :, cols].rearrange("p t (c i) -> p c t i", i=4),
+                ALU.mult,
+            )
+
+        def quantise_z(a, i):
+            cols = halves[i]
+            nc.vector.quantize_mx(
+                out=z_w[a][:, cols].bitcast(FP8X4), scales=z_s[a][:, cols],
+                in_=z_b[a][:, PACK * cols.start : PACK * cols.stop],
+            )
+
+        first_stage(0)
+        features(0, 0)
+        features(0, 1)
+        pick_last(0)
+        pick_change(0)
+        first_stage(1)
+        features(1, 0)
+        features(1, 1)
+        for s in range(1, SLICES - 1):
+            first_stage(s + 1)
+            features(s + 1, 0)
+            pick_last(s)
+            features(s + 1, 1)
+            pick_change(s)
+            make_gate(s - 1, slice(0, PAIRS))
+        make_gate(SLICES - 2, slice(0, PAIRS))
+        z_b[0] = keep.tile([P, PAIRS * PACK], BF16, name="late", align_bytes=64)
+        z_b[1] = keep.tile([P, PAIRS * PACK], BF16, name="z_b1", align_bytes=64)
+        pick_last(SLICES - 1)
+        product(0, 0)
+        pick_change(SLICES - 1)
+        product(0, 1)
+        for cols in halves:
+            make_gate(SLICES - 1, cols)
+        quantise_z(0, 0)
+        product(1, 0)
+        quantise_z(0, 1)
+        product(1, 1)
+        quantise_z(1, 0)
+        quantise_z(1, 1)
+
+        y_banks = {}
+        for i in range(2):
+            for b in range(N_TILES // 2):
+                y_banks[i, b] = psum.tile([P, 2, HALF], F32, name="bank")
+
+        def second_stage(a, i, b):
+            for u in range(2):
+                nt = 2 * b + u
+                for c in range(HALF // MM):
+                    cols = slice(HALF * i + MM * c, HALF * i + MM * (c + 1))
+                    nc.tensor.matmul_mx(
+                        out=y_banks[i, b][:, u, MM * c : MM * (c + 1)],
+                        lhsT=w4_w[:, a, 2 * P * nt : 2 * P * (nt + 1)].bitcast(FP4X4),
+                        lhsT_scale=w4_s[:, a, P * nt : P * (nt + 1)],
+                        rhs=z_w[a][:, cols].bitcast(FP8X4), rhs_scale=z_s[a][:, cols],
+                        start=(a == 0 and u == 0 and c == 0),
+                        stop=(a == PASSES - 1 and u == 1 and c == HALF // MM - 1),
+                    )
+
+        for a in range(PASSES):
+            for i in range(2):
+                for b in range(N_TILES // 2):
+                    second_stage(a, i, b)
+        out_rows = out.rearrange("(nt p) m -> p nt m", p=P)
+        for i in range(2):
+            for b in range(N_TILES // 2):
+                result = ring.tile([P, 2, HALF], F32, name="result", bufs=6)
+                nc.vector.tensor_tensor(result[:], y_banks[i, b][:], base_t[:, 2 * b : 2 * b + 2, halves[i]], ALU.add)
+                nc.sync.dma_start(out_rows[:, 2 * b : 2 * b + 2, halves[i]], result[:])

@@ -47,18 +47,13 @@ def tile_list_audit_schedule_priorities_kernel(
         v_w = [keep.tile([P, BANK], U32, name="v_w%d" % i, align_bytes=64) for i in range(2)]
         v_s_picked = keep.tile([P, S], U8, name="v_s_picked", align_bytes=64)
         v_s = keep.tile([P, S], U8, name="v_s", align_bytes=64)
-        w4_w = keep.tile([P, PASSES, 2 * N], U8, name="w4_w", align_bytes=64)
-        w4_s = keep.tile([P, PASSES, N], U8, name="w4_s", align_bytes=64)
         zero = keep.tile([P, 1], F32, name="zero")
         no_bias = keep.tile([P, 1], F32, name="no_bias")
-        lift_t = keep.tile([P, PASSES, PACK], F32, name="lift_t")
         half_lift = keep.tile([P, PASSES * PACK], F32, name="half_lift")
-        base_t = keep.tile([P, N_TILES, PAIRS], F32, name="base_t")
 
-        nc.vector.memset(tab_s[:].bitcast(I32), 0)
+        nc.gpsimd.memset(tab_s[:].bitcast(I32), 0)
         nc.gpsimd.memset(zero[:], 0.0)
         nc.gpsimd.memset(v_s[:].bitcast(I32), 0)
-        nc.gpsimd.memset(w4_s[:].rearrange("p a c -> p (a c)").bitcast(I32), 0)
         nc.scalar.activation(no_bias[:], zero[:], ACT.Silu)
 
         nc.sync.dma_start(offs_t[:], offs)
@@ -66,34 +61,23 @@ def tile_list_audit_schedule_priorities_kernel(
             r0 = QUADRANT * d + STRADDLE
             nc.sync.dma_start(tab_s[r0 : r0 + 4, :].bitcast(I32), tab_scales[0, 4 * d : 4 * d + 4, :].bitcast(I32))
         w1_rows = w1.rearrange("(p j) c -> p j c", j=PACK)
-        w1_first = [keep.tile([P, PACK, K_PASS // 2], F32, name="w1_first%d" % i) for i in range(2)]
-        nc.sync.dma_start(w1_first[0][:], w1_rows[:, :, 0:256])
+        w1_raw = [keep.tile([P, PACK, 256], F32, name="w1_raw%d" % i, align_bytes=64) for i in range(3)]
+        nc.sync.dma_start(w1_raw[0][:], w1_rows[:, :, 0:256])
         nc.sync.dma_start(tab_w[:], tab_words[0].rearrange("p t i -> p (t i)").bitcast(I32))
-        nc.sync.dma_start(w1_first[1][:], w1_rows[:, :, 256:512])
-
-        nc.vector.tensor_copy(v_s_picked[:], tab_s[:].indirect(offs_t[:]))
-        for d in range(4):
-            r0 = QUADRANT * d
-            nc.sync.dma_start(
-                v_s[r0 : r0 + 4, :].bitcast(I32), v_s_picked[r0 + STRADDLE : r0 + STRADDLE + 4, :].bitcast(I32)
-            )
-
-        w1_second = keep.tile([P, PACK, K_PASS], F32, name="w1_second")
-        nc.sync.dma_start(w1_second[:], w1_rows[:, :, K_PASS:])
+        nc.sync.dma_start(w1_raw[1][:], w1_rows[:, :, 256:512])
+        nc.sync.dma_start(w1_raw[2][:], w1_rows[:, :, 512:768])
         nc.sync.dma_start(pos2_t[:], pos2)
         nc.sync.dma_start(pos1_t[:], pos1)
-        nc.sync.dma_start(lift_t[:], lift.rearrange("(a p t) -> p a t", p=P, t=PACK))
-        nc.sync.dma_start(w4_w[:].bitcast(I32), w4_words.rearrange("a p c -> p a c").bitcast(I32))
-        for d in range(4):
-            r0 = QUADRANT * d
-            nc.sync.dma_start(
-                w4_s[r0 : r0 + 4, :, :].bitcast(I32),
-                w4_scales[:, 4 * d : 4 * d + 4, :].rearrange("a q c -> q a c").bitcast(I32),
-            )
-        nc.sync.dma_start(base_t[:], base.rearrange("(nt p) m -> p nt m", p=P))
-        nc.gpsimd.tensor_scalar(half_lift[:], lift_t[:].rearrange("p a t -> p (a t)"), 0.5, 0.0, ALU.mult, ALU.add)
 
-        w1_b = [keep.tile([P, PACK, P, PACK], BF16, name="w1_b%d" % a, align_bytes=64) for a in range(PASSES)]
+        nc.vector.tensor_copy(v_s_picked[:], tab_s[:].indirect(offs_t[:]))
+        for r0, rows in ((0, 4), (QUADRANT, 2 * QUADRANT), (3 * QUADRANT, 4)):
+            nc.sync.dma_start(
+                v_s[r0 : r0 + rows, :].bitcast(I32), v_s_picked[r0 + STRADDLE : r0 + STRADDLE + rows, :].bitcast(I32)
+            )
+        w1_raw.append(keep.tile([P, PACK, 256], F32, name="tab_s", align_bytes=64))
+        nc.sync.dma_start(w1_raw[3][:], w1_rows[:, :, 768:1024])
+
+        w1_b = [keep.tile([P, PACK, P, PACK], BF16, name="w1_b", align_bytes=64)]
         w1_w = [keep.tile([P, K_PASS], U32, name="w1_w%d" % a, align_bytes=64) for a in range(PASSES)]
         w1_s = [keep.tile([P, K_PASS], U8, name="w1_s%d" % a, align_bytes=64) for a in range(PASSES)]
 
@@ -104,25 +88,44 @@ def tile_list_audit_schedule_priorities_kernel(
                 in_=w1_b[a][:, t0:t1, :, :].rearrange("p t m j -> p (t m j)"),
             )
 
-        for i in range(2):
-            nc.scalar.copy(
-                w1_b[0][:, :, 64 * i : 64 * (i + 1), :].rearrange("p t m j -> p m j t"),
-                w1_first[i][:].rearrange("p j (m t) -> p m j t", t=PACK),
+        def deal_w1(copy, a, i, raw):
+            copy(
+                w1_b[a][:, :, 64 * i : 64 * (i + 1), :].rearrange("p t m j -> p m j t"),
+                raw[:].rearrange("p j (m t) -> p m j t", t=PACK),
             )
+
+        for i in range(2):
+            deal_w1(nc.scalar.copy, 0, i, w1_raw[i])
         for i in range(2):
             nc.vector.tensor_copy(v_w[i][:], tab_w[:].bitcast(U32).indirect(offs_t[:, 32 * i : 32 * (i + 1)]))
         quantise_w1(0, 0, 2)
         quantise_w1(0, 2, 4)
-        nc.vector.tensor_copy(
-            w1_b[1][:].rearrange("p t m j -> p m j t"), w1_second[:].rearrange("p j (m t) -> p m j t", t=PACK)
-        )
+        w1_b.append(keep.tile([P, PACK, P, PACK], BF16, name="w1_b", align_bytes=64))
+        for i in range(2):
+            deal_w1(nc.vector.tensor_copy, 1, i, w1_raw[2 + i])
         quantise_w1(1, 0, 4)
+
+        lift_t = keep.tile([P, PASSES, PACK], F32, name="v_s_picked", align_bytes=64)
+        w4_s = keep.tile([P, PASSES, N], U8, name="w1_raw0", align_bytes=64)
+        w4_w = keep.tile([P, PASSES, 2 * N], U8, name="w1_raw1", align_bytes=64)
+        base_t = keep.tile([P, N_TILES, PAIRS], F32, name="tab_w", align_bytes=64)
+        nc.gpsimd.memset(w4_s[:].rearrange("p a c -> p (a c)").bitcast(I32), 0)
+        nc.sync.dma_start(lift_t[:], lift.rearrange("(a p t) -> p a t", p=P, t=PACK))
+        nc.gpsimd.tensor_scalar(half_lift[:], lift_t[:].rearrange("p a t -> p (a t)"), 0.5, 0.0, ALU.mult, ALU.add)
+        for d in range(4):
+            r0 = QUADRANT * d
+            nc.sync.dma_start(
+                w4_s[r0 : r0 + 4, :, :].bitcast(I32),
+                w4_scales[:, 4 * d : 4 * d + 4, :].rearrange("a q c -> q a c").bitcast(I32),
+            )
+        nc.sync.dma_start(w4_w[:].bitcast(I32), w4_words.rearrange("a p c -> p a c").bitcast(I32))
+        nc.sync.dma_start(base_t[:], base.rearrange("(nt p) m -> p nt m", p=P))
 
         last = [keep.tile([P, PACK, PAIRS], F32, name="last%d" % a) for a in range(PASSES)]
         gate = [keep.tile([P, PACK, PAIRS], F32, name="gate%d" % a) for a in range(PASSES)]
         first_sines = keep.tile([P, 2, BANK], F32, name="first_sines")
         z_b = {}
-        z_w = [keep.tile([P, PAIRS], U32, name="z_w%d" % a, align_bytes=64) for a in range(PASSES)]
+        z_w = {}
         z_s = [keep.tile([P, PAIRS], U8, name="z_s%d" % a, align_bytes=64) for a in range(PASSES)]
         a_banks, squares, h_tiles = {}, {}, {}
 
@@ -142,15 +145,21 @@ def tile_list_audit_schedule_priorities_kernel(
                     out=bank[:], lhsT=w1_w[a][:, cols].bitcast(FP8X4), lhsT_scale=w1_s[a][:, cols],
                     rhs=v_w[i][:].bitcast(FP8X4), rhs_scale=v_s[:, BANK * i : BANK * (i + 1)], start=True, stop=True,
                 )
-            for i in range(2):
+            def sine(i):
                 nc.scalar.activation(sine_slot(s, i), a_banks[s, i][:], ACT.Sin, bias=no_bias[:], scale=0.5)
-            for i in range(2):
+
+            def square(i):
                 if (s, i) == (SLICES - 1, 1):
                     squares[s, i] = keep.tile([P, BANK], F32, name="late", align_bytes=64)
                 else:
                     squares[s, i] = ring.tile([P, BANK], F32, name="square", bufs=4)
                 nc.scalar.activation(squares[s, i][:], sine_slot(s, i), ACT.Square, scale=math.sqrt(2.0))
-            h_tiles[s] = ring.tile([P, S], F32, name="h")
+
+            for i in range(2):
+                sine(i)
+            for i in range(2):
+                square(i)
+            h_tiles[s] = keep.tile([P, S], F32, name="h%d" % s, align_bytes=64)
 
         def features(s, i):
             nc.vector.scalar_tensor_tensor(
@@ -173,22 +182,19 @@ def tile_list_audit_schedule_priorities_kernel(
 
         halves = [slice(HALF * i, HALF * (i + 1)) for i in range(2)]
 
-        def product(a, i):
-            cols = halves[i]
-            nc.vector.tensor_tensor(
-                z_b[a][:, PACK * cols.start : PACK * cols.stop].rearrange("p (c i t) -> p c t i", i=4, t=PACK),
+        def product(engine, a, cols, z):
+            engine.tensor_tensor(
+                z.rearrange("p (c i t) -> p c t i", i=4, t=PACK),
                 gate[a][:, :, cols].rearrange("p t (c i) -> p c t i", i=4),
                 last[a][:, :, cols].rearrange("p t (c i) -> p c t i", i=4),
                 ALU.mult,
             )
 
-        def quantise_z(a, i):
-            cols = halves[i]
-            nc.vector.quantize_mx(
-                out=z_w[a][:, cols].bitcast(FP8X4), scales=z_s[a][:, cols],
-                in_=z_b[a][:, PACK * cols.start : PACK * cols.stop],
-            )
+        def quantise_z(a, cols, z):
+            nc.vector.quantize_mx(out=z_w[a][:, cols].bitcast(FP8X4), scales=z_s[a][:, cols], in_=z)
 
+        quarters = [slice(MM * i, MM * (i + 1)) for i in range(4)]
+        z0 = {}
         first_stage(0)
         features(0, 0)
         features(0, 1)
@@ -203,22 +209,35 @@ def tile_list_audit_schedule_priorities_kernel(
             pick_last(s)
             features(s + 1, 1)
             pick_change(s)
-            make_gate(s - 1, slice(0, PAIRS))
+            if s == PACK:
+                make_gate(s - 1, quarters[0])
+                z0[0] = keep.tile([P, MM * PACK], BF16, name="z0_first", align_bytes=64)
+                product(nc.gpsimd, 0, quarters[0], z0[0][:])
+                make_gate(s - 1, slice(MM, PAIRS))
+            else:
+                make_gate(s - 1, slice(0, PAIRS))
+            if s in (PACK, PACK + 1):
+                q = s - PACK + 1
+                z0[q] = keep.tile([P, MM * PACK], BF16, name="h%d" % s, align_bytes=64)
+                product(nc.gpsimd, 0, quarters[q], z0[q][:])
         make_gate(SLICES - 2, slice(0, PAIRS))
-        z_b[0] = keep.tile([P, PAIRS * PACK], BF16, name="late", align_bytes=64)
-        z_b[1] = keep.tile([P, PAIRS * PACK], BF16, name="z_b1", align_bytes=64)
+        z_w[0] = keep.tile([P, PAIRS], U32, name="late", align_bytes=64)
+        z_w[1] = keep.tile([P, PAIRS], U32, name="z_w1", align_bytes=64)
+        z0[3] = keep.tile([P, MM * PACK], BF16, name="h%d" % (SLICES - 2), align_bytes=64)
+        z1 = keep.tile([P, PAIRS * PACK], BF16, name="z1", align_bytes=64)
+        z1_halves = [z1[:, PACK * cols.start : PACK * cols.stop] for cols in halves]
         pick_last(SLICES - 1)
-        product(0, 0)
+        quantise_z(0, quarters[0], z0[0][:])
+        quantise_z(0, quarters[1], z0[1][:])
         pick_change(SLICES - 1)
-        product(0, 1)
+        product(nc.vector, 0, quarters[3], z0[3][:])
         for cols in halves:
             make_gate(SLICES - 1, cols)
-        quantise_z(0, 0)
-        product(1, 0)
-        quantise_z(0, 1)
-        product(1, 1)
-        quantise_z(1, 0)
-        quantise_z(1, 1)
+        quantise_z(0, quarters[2], z0[2][:])
+        product(nc.vector, 1, halves[0], z1_halves[0])
+        quantise_z(0, quarters[3], z0[3][:])
+        quantise_z(1, halves[0], z1_halves[0])
+        product(nc.vector, 1, halves[1], z1_halves[1])
 
         y_banks = {}
         for i in range(2):
@@ -239,13 +258,23 @@ def tile_list_audit_schedule_priorities_kernel(
                         stop=(a == PASSES - 1 and u == 1 and c == HALF // MM - 1),
                     )
 
-        for a in range(PASSES):
-            for i in range(2):
-                for b in range(N_TILES // 2):
-                    second_stage(a, i, b)
         out_rows = out.rearrange("(nt p) m -> p nt m", p=P)
-        for i in range(2):
+
+        def finish(i, b):
+            result = ring.tile([P, 2, HALF], F32, name="result", bufs=6)
+            nc.vector.tensor_tensor(result[:], y_banks[i, b][:], base_t[:, 2 * b : 2 * b + 2, halves[i]], ALU.add)
+            nc.sync.dma_start(out_rows[:, 2 * b : 2 * b + 2, halves[i]], result[:])
+
+        for a in range(PASSES):
             for b in range(N_TILES // 2):
-                result = ring.tile([P, 2, HALF], F32, name="result", bufs=6)
-                nc.vector.tensor_tensor(result[:], y_banks[i, b][:], base_t[:, 2 * b : 2 * b + 2, halves[i]], ALU.add)
-                nc.sync.dma_start(out_rows[:, 2 * b : 2 * b + 2, halves[i]], result[:])
+                second_stage(a, 0, b)
+        for b in range(N_TILES // 2):
+            second_stage(0, 1, b)
+        finish(0, 0)
+        quantise_z(1, halves[1], z1_halves[1])
+        for b in range(N_TILES // 2):
+            second_stage(1, 1, b)
+        finish(0, 1)
+        finish(0, 2)
+        for b in range(N_TILES // 2):
+            finish(1, b)

@@ -21,13 +21,18 @@ P = 128
 PACK = 4
 K_PASS = P * PACK
 BANK = 512
+GROUP = 16
 QUADRANT = 32
-STRADDLE = 14
+SCALE_ROWS = 4
+STRADDLE = GROUP - SCALE_ROWS // 2
 PASSES = H // K_PASS
 SLICES = H // P
+LAST = SLICES - 1
 N_TILES = N // P
+W1_PIECE = 256
 HALF = PAIRS // 2
-MM = 128
+QUARTER = PAIRS // 4
+SHARES = (slice(0, 128), slice(128, 320), slice(320, 512))
 
 
 def tile_list_audit_schedule_priorities_kernel(
@@ -36,20 +41,23 @@ def tile_list_audit_schedule_priorities_kernel(
     nc = tc.nc
     with ExitStack() as ctx:
         keep = ctx.enter_context(tc.tile_pool(name="keep", bufs=1))
-        ring = ctx.enter_context(tc.tile_pool(name="ring", bufs=3))
+        ring = ctx.enter_context(tc.tile_pool(name="ring", bufs=1))
         psum = ctx.enter_context(tc.psum_pool(name="psum", bufs=8))
 
-        offs_t = keep.tile([P, S // 16], U16, name="offs_t")
-        pos1_t = keep.tile([P, PAIRS // 16], U16, name="pos1_t")
-        pos2_t = keep.tile([P, PAIRS // 16], U16, name="pos2_t")
-        tab_w = keep.tile([P, T], I32, name="tab_w", align_bytes=64)
-        tab_s = keep.tile([P, T], U8, name="tab_s", align_bytes=64)
-        v_w = [keep.tile([P, BANK], U32, name="v_w%d" % i, align_bytes=64) for i in range(2)]
-        v_s_picked = keep.tile([P, S], U8, name="v_s_picked", align_bytes=64)
-        v_s = keep.tile([P, S], U8, name="v_s", align_bytes=64)
+        def held(shape, dtype, name):
+            return keep.tile(shape, dtype, name=name, align_bytes=64)
+
+        offs_t = keep.tile([P, S // GROUP], U16, name="offs_t")
+        pos1_t = keep.tile([P, PAIRS // GROUP], U16, name="pos1_t")
+        pos2_t = keep.tile([P, PAIRS // GROUP], U16, name="pos2_t")
+        tab_w = held([P, T], I32, "tab_w")
+        tab_s = held([P, T], U8, "tab_s")
+        v_w = [held([P, BANK], U32, "v_w%d" % i) for i in range(2)]
+        v_s_picked = held([P, S], U8, "v_s_picked")
+        v_s = held([P, S], U8, "v_s")
         zero = keep.tile([P, 1], F32, name="zero")
         no_bias = keep.tile([P, 1], F32, name="no_bias")
-        half_lift = keep.tile([P, PASSES * PACK], F32, name="half_lift")
+        half_lift = keep.tile([P, SLICES], F32, name="half_lift")
 
         nc.gpsimd.memset(tab_s[:].bitcast(I32), 0)
         nc.gpsimd.memset(zero[:], 0.0)
@@ -57,224 +65,233 @@ def tile_list_audit_schedule_priorities_kernel(
         nc.scalar.activation(no_bias[:], zero[:], ACT.Silu)
 
         nc.sync.dma_start(offs_t[:], offs)
-        for d in range(4):
+        for d in range(P // QUADRANT):
             r0 = QUADRANT * d + STRADDLE
-            nc.sync.dma_start(tab_s[r0 : r0 + 4, :].bitcast(I32), tab_scales[0, 4 * d : 4 * d + 4, :].bitcast(I32))
+            rows = tab_scales[0, SCALE_ROWS * d : SCALE_ROWS * (d + 1), :]
+            nc.sync.dma_start(tab_s[r0 : r0 + SCALE_ROWS, :].bitcast(I32), rows.bitcast(I32))
         w1_rows = w1.rearrange("(p j) c -> p j c", j=PACK)
-        w1_raw = [keep.tile([P, PACK, 256], F32, name="w1_raw%d" % i, align_bytes=64) for i in range(3)]
-        nc.sync.dma_start(w1_raw[0][:], w1_rows[:, :, 0:256])
+        w1_raw = {}
+
+        def load_w1(piece, name):
+            w1_raw[piece] = held([P, PACK, W1_PIECE], F32, name)
+            nc.sync.dma_start(w1_raw[piece][:], w1_rows[:, :, W1_PIECE * piece : W1_PIECE * (piece + 1)])
+
+        load_w1(0, "w1_raw0")
         nc.sync.dma_start(tab_w[:], tab_words[0].rearrange("p t i -> p (t i)").bitcast(I32))
-        nc.sync.dma_start(w1_raw[1][:], w1_rows[:, :, 256:512])
-        nc.sync.dma_start(w1_raw[2][:], w1_rows[:, :, 512:768])
+        load_w1(1, "w1_raw1")
+        load_w1(2, "w1_raw2")
         nc.sync.dma_start(pos2_t[:], pos2)
         nc.sync.dma_start(pos1_t[:], pos1)
 
         nc.vector.tensor_copy(v_s_picked[:], tab_s[:].indirect(offs_t[:]))
-        for r0, rows in ((0, 4), (QUADRANT, 2 * QUADRANT), (3 * QUADRANT, 4)):
+        for r0, count in ((0, SCALE_ROWS), (QUADRANT, 2 * QUADRANT), (3 * QUADRANT, SCALE_ROWS)):
             nc.sync.dma_start(
-                v_s[r0 : r0 + rows, :].bitcast(I32), v_s_picked[r0 + STRADDLE : r0 + STRADDLE + rows, :].bitcast(I32)
+                v_s[r0 : r0 + count, :].bitcast(I32), v_s_picked[r0 + STRADDLE : r0 + STRADDLE + count, :].bitcast(I32)
             )
-        w1_raw.append(keep.tile([P, PACK, 256], F32, name="tab_s", align_bytes=64))
-        nc.sync.dma_start(w1_raw[3][:], w1_rows[:, :, 768:1024])
+        load_w1(3, "tab_s")
 
-        w1_b = [keep.tile([P, PACK, P, PACK], BF16, name="w1_b", align_bytes=64)]
-        w1_w = [keep.tile([P, K_PASS], U32, name="w1_w%d" % a, align_bytes=64) for a in range(PASSES)]
-        w1_s = [keep.tile([P, K_PASS], U8, name="w1_s%d" % a, align_bytes=64) for a in range(PASSES)]
+        w1_w = [held([P, K_PASS], U32, "w1_w%d" % a) for a in range(PASSES)]
+        w1_s = [held([P, K_PASS], U8, "w1_s%d" % a) for a in range(PASSES)]
 
-        def quantise_w1(a, t0, t1):
+        def deal_w1(copy, dealt, piece):
+            m_count = W1_PIECE // PACK
+            m0 = m_count * piece % P
+            copy(
+                dealt[:, :, m0 : m0 + m_count, :].rearrange("p t m j -> p m j t"),
+                w1_raw[piece][:].rearrange("p j (m t) -> p m j t", t=PACK),
+            )
+
+        def quantise_w1(a, dealt, t0, t1):
             cols = slice(P * t0, P * t1)
             nc.vector.quantize_mx(
-                out=w1_w[a][:, cols].bitcast(FP8X4), scales=w1_s[a][:, cols],
-                in_=w1_b[a][:, t0:t1, :, :].rearrange("p t m j -> p (t m j)"),
+                out=w1_w[a][:, cols].bitcast(FP8X4),
+                scales=w1_s[a][:, cols],
+                in_=dealt[:, t0:t1, :, :].rearrange("p t m j -> p (t m j)"),
             )
 
-        def deal_w1(copy, a, i, raw):
-            copy(
-                w1_b[a][:, :, 64 * i : 64 * (i + 1), :].rearrange("p t m j -> p m j t"),
-                raw[:].rearrange("p j (m t) -> p m j t", t=PACK),
-            )
+        dealt = held([P, PACK, P, PACK], BF16, "dealt")
+        for piece in (0, 1):
+            deal_w1(nc.scalar.copy, dealt, piece)
+        for i in range(2):
+            entries = offs_t[:, BANK // GROUP * i : BANK // GROUP * (i + 1)]
+            nc.vector.tensor_copy(v_w[i][:], tab_w[:].bitcast(U32).indirect(entries))
+        quantise_w1(0, dealt, 0, 2)
+        quantise_w1(0, dealt, 2, 4)
+        dealt = held([P, PACK, P, PACK], BF16, "dealt")
+        for piece in (2, 3):
+            deal_w1(nc.vector.tensor_copy, dealt, piece)
+        quantise_w1(1, dealt, 0, 4)
 
-        for i in range(2):
-            deal_w1(nc.scalar.copy, 0, i, w1_raw[i])
-        for i in range(2):
-            nc.vector.tensor_copy(v_w[i][:], tab_w[:].bitcast(U32).indirect(offs_t[:, 32 * i : 32 * (i + 1)]))
-        quantise_w1(0, 0, 2)
-        quantise_w1(0, 2, 4)
-        w1_b.append(keep.tile([P, PACK, P, PACK], BF16, name="w1_b", align_bytes=64))
-        for i in range(2):
-            deal_w1(nc.vector.tensor_copy, 1, i, w1_raw[2 + i])
-        quantise_w1(1, 0, 4)
-
-        lift_t = keep.tile([P, PASSES, PACK], F32, name="v_s_picked", align_bytes=64)
-        w4_s = keep.tile([P, PASSES, N], U8, name="w1_raw0", align_bytes=64)
-        w4_w = keep.tile([P, PASSES, 2 * N], U8, name="w1_raw1", align_bytes=64)
-        base_t = keep.tile([P, N_TILES, PAIRS], F32, name="tab_w", align_bytes=64)
+        lift_t = held([P, PASSES, PACK], F32, "v_s_picked")
+        w4_s = held([P, PASSES, N], U8, "w1_raw0")
+        w4_w = held([P, PASSES, 2 * N], U8, "w1_raw1")
+        base_t = held([P, N_TILES, PAIRS], F32, "tab_w")
         nc.gpsimd.memset(w4_s[:].rearrange("p a c -> p (a c)").bitcast(I32), 0)
         nc.sync.dma_start(lift_t[:], lift.rearrange("(a p t) -> p a t", p=P, t=PACK))
         nc.gpsimd.tensor_scalar(half_lift[:], lift_t[:].rearrange("p a t -> p (a t)"), 0.5, 0.0, ALU.mult, ALU.add)
-        for d in range(4):
-            r0 = QUADRANT * d
-            nc.sync.dma_start(
-                w4_s[r0 : r0 + 4, :, :].bitcast(I32),
-                w4_scales[:, 4 * d : 4 * d + 4, :].rearrange("a q c -> q a c").bitcast(I32),
-            )
+        for d in range(P // QUADRANT):
+            rows = w4_scales[:, SCALE_ROWS * d : SCALE_ROWS * (d + 1), :].rearrange("a q c -> q a c")
+            nc.sync.dma_start(w4_s[QUADRANT * d : QUADRANT * d + SCALE_ROWS, :, :].bitcast(I32), rows.bitcast(I32))
         nc.sync.dma_start(w4_w[:].bitcast(I32), w4_words.rearrange("a p c -> p a c").bitcast(I32))
         nc.sync.dma_start(base_t[:], base.rearrange("(nt p) m -> p nt m", p=P))
 
-        last = [keep.tile([P, PACK, PAIRS], F32, name="last%d" % a) for a in range(PASSES)]
+        last_year = [keep.tile([P, PACK, PAIRS], F32, name="last_year%d" % a) for a in range(PASSES)]
         gate = [keep.tile([P, PACK, PAIRS], F32, name="gate%d" % a) for a in range(PASSES)]
         first_sines = keep.tile([P, 2, BANK], F32, name="first_sines")
-        z_b = {}
-        z_w = {}
-        z_s = [keep.tile([P, PAIRS], U8, name="z_s%d" % a, align_bytes=64) for a in range(PASSES)]
-        a_banks, squares, h_tiles = {}, {}, {}
+        z_s = [held([P, PAIRS], U8, "z_s%d" % a) for a in range(PASSES)]
+        a_banks, squares, h_tiles, z_w, z_shares = {}, {}, {}, {}, {}
+        halves = [slice(HALF * i, HALF * (i + 1)) for i in range(2)]
+        quarters = [slice(QUARTER * i, QUARTER * (i + 1)) for i in range(4)]
 
-        def sine_slot(s, i):
+        def sines(s, i):
             if s <= 1:
                 return first_sines[:, i, :]
             a, t = divmod(s - 1, PACK)
-            return (last, gate)[i][a][:, t, :]
+            return (last_year, gate)[i][a][:, t, :]
 
-        def first_stage(s):
+        def first_product(s):
             a, t = divmod(s, PACK)
             cols = slice(P * t, P * (t + 1))
             for i in range(2):
-                bank = psum.tile([P, BANK], F32, name="bank")
-                a_banks[s, i] = bank
+                a_banks[s, i] = psum.tile([P, BANK], F32, name="bank")
                 nc.tensor.matmul_mx(
-                    out=bank[:], lhsT=w1_w[a][:, cols].bitcast(FP8X4), lhsT_scale=w1_s[a][:, cols],
-                    rhs=v_w[i][:].bitcast(FP8X4), rhs_scale=v_s[:, BANK * i : BANK * (i + 1)], start=True, stop=True,
+                    out=a_banks[s, i][:],
+                    lhsT=w1_w[a][:, cols].bitcast(FP8X4),
+                    lhsT_scale=w1_s[a][:, cols],
+                    rhs=v_w[i][:].bitcast(FP8X4),
+                    rhs_scale=v_s[:, BANK * i : BANK * (i + 1)],
+                    start=True,
+                    stop=True,
                 )
-            def sine(i):
-                nc.scalar.activation(sine_slot(s, i), a_banks[s, i][:], ACT.Sin, bias=no_bias[:], scale=0.5)
-
-            def square(i):
-                if (s, i) == (SLICES - 1, 1):
-                    squares[s, i] = keep.tile([P, BANK], F32, name="late", align_bytes=64)
-                else:
-                    squares[s, i] = ring.tile([P, BANK], F32, name="square", bufs=4)
-                nc.scalar.activation(squares[s, i][:], sine_slot(s, i), ACT.Square, scale=math.sqrt(2.0))
-
             for i in range(2):
-                sine(i)
+                nc.scalar.activation(sines(s, i), a_banks[s, i][:], ACT.Sin, bias=no_bias[:], scale=0.5)
             for i in range(2):
-                square(i)
-            h_tiles[s] = keep.tile([P, S], F32, name="h%d" % s, align_bytes=64)
+                squares[s, i] = ring.tile([P, BANK], F32, name="square", bufs=4)
+                nc.scalar.activation(squares[s, i][:], sines(s, i), ACT.Square, scale=math.sqrt(2.0))
+            h_tiles[s] = held([P, S], F32, "h%d" % s)
 
         def features(s, i):
             nc.vector.scalar_tensor_tensor(
                 h_tiles[s][:, BANK * i : BANK * (i + 1)], a_banks[s, i][:], 1.0, squares[s, i][:], ALU.add, ALU.subtract
             )
 
-        def pick_last(s):
+        def pick_last_year(s):
             a, t = divmod(s, PACK)
-            nc.vector.tensor_copy(last[a][:, t, :], h_tiles[s][:].indirect(pos2_t[:]))
+            nc.vector.tensor_copy(last_year[a][:, t, :], h_tiles[s][:].indirect(pos2_t[:]))
 
-        def pick_change(s):
+        def pick_difference(s, cols):
             a, t = divmod(s, PACK)
-            nc.vector.tensor_tensor(gate[a][:, t, :], h_tiles[s][:].indirect(pos1_t[:]), last[a][:, t, :], ALU.subtract)
+            this_year = h_tiles[s][:].indirect(pos1_t[:, cols.start // GROUP : cols.stop // GROUP])
+            nc.vector.tensor_tensor(gate[a][:, t, cols], this_year, last_year[a][:, t, cols], ALU.subtract)
 
-        def make_gate(s, cols):
+        def make_gate(s, *pieces):
             a, t = divmod(s, PACK)
-            g = gate[a][:, t, cols]
-            nc.scalar.activation(g, g, ACT.Tanh, scale=0.5)
-            nc.scalar.activation(g, g, ACT.Identity, bias=half_lift[:, s : s + 1], scale=half_lift[:, s : s + 1])
+            factor = half_lift[:, s : s + 1]
+            for cols in pieces:
+                nc.scalar.activation(gate[a][:, t, cols], gate[a][:, t, cols], ACT.Tanh, scale=0.5)
+            for cols in pieces:
+                nc.scalar.activation(gate[a][:, t, cols], gate[a][:, t, cols], ACT.Identity, bias=factor, scale=factor)
 
-        halves = [slice(HALF * i, HALF * (i + 1)) for i in range(2)]
-
-        def product(engine, a, cols, z):
+        def make_z(engine, a, cols, z):
             engine.tensor_tensor(
-                z.rearrange("p (c i t) -> p c t i", i=4, t=PACK),
+                z[:].rearrange("p (c i t) -> p c t i", i=4, t=PACK),
                 gate[a][:, :, cols].rearrange("p t (c i) -> p c t i", i=4),
-                last[a][:, :, cols].rearrange("p t (c i) -> p c t i", i=4),
+                last_year[a][:, :, cols].rearrange("p t (c i) -> p c t i", i=4),
                 ALU.mult,
             )
 
         def quantise_z(a, cols, z):
             nc.vector.quantize_mx(out=z_w[a][:, cols].bitcast(FP8X4), scales=z_s[a][:, cols], in_=z)
 
-        quarters = [slice(MM * i, MM * (i + 1)) for i in range(4)]
-        z0 = {}
-        first_stage(0)
+        def make_share(q, name):
+            z_shares[q] = held([P, PACK * (SHARES[q].stop - SHARES[q].start)], BF16, name)
+            make_z(nc.gpsimd, 0, SHARES[q], z_shares[q])
+
+        def quantise_share(q, start, stop):
+            c0 = SHARES[q].start
+            quantise_z(0, slice(start, stop), z_shares[q][:, PACK * (start - c0) : PACK * (stop - c0)])
+
+        every_pair = slice(0, PAIRS)
+        first_product(0)
         features(0, 0)
         features(0, 1)
-        pick_last(0)
-        pick_change(0)
-        first_stage(1)
+        pick_last_year(0)
+        pick_difference(0, every_pair)
+        first_product(1)
         features(1, 0)
         features(1, 1)
-        for s in range(1, SLICES - 1):
-            first_stage(s + 1)
+        for s in range(1, LAST):
+            first_product(s + 1)
             features(s + 1, 0)
-            pick_last(s)
+            pick_last_year(s)
             features(s + 1, 1)
-            pick_change(s)
-            if s == PACK:
-                make_gate(s - 1, quarters[0])
-                z0[0] = keep.tile([P, MM * PACK], BF16, name="z0_first", align_bytes=64)
-                product(nc.gpsimd, 0, quarters[0], z0[0][:])
-                make_gate(s - 1, slice(MM, PAIRS))
+            pick_difference(s, every_pair)
+            if s - 1 == PACK - 1:
+                make_gate(s - 1, SHARES[0])
+                make_share(0, "z_share0")
+                make_gate(s - 1, slice(SHARES[0].stop, PAIRS))
             else:
-                make_gate(s - 1, slice(0, PAIRS))
+                make_gate(s - 1, every_pair)
             if s in (PACK, PACK + 1):
-                q = s - PACK + 1
-                z0[q] = keep.tile([P, MM * PACK], BF16, name="h%d" % s, align_bytes=64)
-                product(nc.gpsimd, 0, quarters[q], z0[q][:])
-        make_gate(SLICES - 2, slice(0, PAIRS))
-        z_w[0] = keep.tile([P, PAIRS], U32, name="late", align_bytes=64)
-        z_w[1] = keep.tile([P, PAIRS], U32, name="z_w1", align_bytes=64)
-        z0[3] = keep.tile([P, MM * PACK], BF16, name="h%d" % (SLICES - 2), align_bytes=64)
-        z1 = keep.tile([P, PAIRS * PACK], BF16, name="z1", align_bytes=64)
-        z1_halves = [z1[:, PACK * cols.start : PACK * cols.stop] for cols in halves]
-        pick_last(SLICES - 1)
-        quantise_z(0, quarters[0], z0[0][:])
-        quantise_z(0, quarters[1], z0[1][:])
-        pick_change(SLICES - 1)
-        product(nc.vector, 0, quarters[3], z0[3][:])
+                make_share(s - PACK + 1, "h%d" % s)
+        make_gate(LAST - 1, every_pair)
+
+        z_w[0] = held([P, PAIRS], U32, "h%d" % (LAST - 1))
+        z_w[1] = held([P, PAIRS], U32, "z_w1")
+        z_quarters = [held([P, PACK * QUARTER], BF16, "z_quarter%d" % q) for q in range(4)]
+        pick_last_year(LAST)
+        quantise_share(0, 0, 128)
+        quantise_share(1, 128, 256)
         for cols in halves:
-            make_gate(SLICES - 1, cols)
-        quantise_z(0, quarters[2], z0[2][:])
-        product(nc.vector, 1, halves[0], z1_halves[0])
-        quantise_z(0, quarters[3], z0[3][:])
-        quantise_z(1, halves[0], z1_halves[0])
-        product(nc.vector, 1, halves[1], z1_halves[1])
+            pick_difference(LAST, cols)
+        make_gate(LAST, quarters[0], quarters[1])
+        make_gate(LAST, quarters[2], quarters[3])
+        quantise_share(1, 256, 320)
+        quantise_share(2, 320, 384)
+        quantise_share(2, 384, 512)
 
-        y_banks = {}
-        for i in range(2):
-            for b in range(N_TILES // 2):
-                y_banks[i, b] = psum.tile([P, 2, HALF], F32, name="bank")
+        banks = range(N_TILES // 2)
+        y_banks = {(i, b): psum.tile([P, 2, HALF], F32, name="bank") for i in range(2) for b in banks}
 
-        def second_stage(a, i, b):
-            for u in range(2):
-                nt = 2 * b + u
-                for c in range(HALF // MM):
-                    cols = slice(HALF * i + MM * c, HALF * i + MM * (c + 1))
-                    nc.tensor.matmul_mx(
-                        out=y_banks[i, b][:, u, MM * c : MM * (c + 1)],
-                        lhsT=w4_w[:, a, 2 * P * nt : 2 * P * (nt + 1)].bitcast(FP4X4),
-                        lhsT_scale=w4_s[:, a, P * nt : P * (nt + 1)],
-                        rhs=z_w[a][:, cols].bitcast(FP8X4), rhs_scale=z_s[a][:, cols],
-                        start=(a == 0 and u == 0 and c == 0),
-                        stop=(a == PASSES - 1 and u == 1 and c == HALF // MM - 1),
-                    )
+        def second_product(a, i):
+            for b in banks:
+                for c in range(2):
+                    cols = quarters[2 * i + c]
+                    for u in range(2):
+                        nt = 2 * b + u
+                        nc.tensor.matmul_mx(
+                            out=y_banks[i, b][:, u, QUARTER * c : QUARTER * (c + 1)],
+                            lhsT=w4_w[:, a, 2 * P * nt : 2 * P * (nt + 1)].bitcast(FP4X4),
+                            lhsT_scale=w4_s[:, a, P * nt : P * (nt + 1)],
+                            rhs=z_w[a][:, cols].bitcast(FP8X4),
+                            rhs_scale=z_s[a][:, cols],
+                            start=(a, c, u) == (0, 0, 0),
+                            stop=(a, c, u) == (PASSES - 1, 1, 1),
+                        )
 
         out_rows = out.rearrange("(nt p) m -> p nt m", p=P)
 
-        def finish(i, b):
-            result = ring.tile([P, 2, HALF], F32, name="result", bufs=6)
-            nc.vector.tensor_tensor(result[:], y_banks[i, b][:], base_t[:, 2 * b : 2 * b + 2, halves[i]], ALU.add)
-            nc.sync.dma_start(out_rows[:, 2 * b : 2 * b + 2, halves[i]], result[:])
+        def finish(i, b, u0=0, u1=2):
+            tiles = slice(2 * b + u0, 2 * b + u1)
+            result = held([P, u1 - u0, HALF], F32, "result%d_%d" % (i, tiles.start))
+            nc.vector.tensor_tensor(result[:], y_banks[i, b][:, u0:u1, :], base_t[:, tiles, halves[i]], ALU.add)
+            nc.sync.dma_start(out_rows[:, tiles, halves[i]], result[:])
 
-        for a in range(PASSES):
-            for b in range(N_TILES // 2):
-                second_stage(a, 0, b)
-        for b in range(N_TILES // 2):
-            second_stage(0, 1, b)
-        finish(0, 0)
-        quantise_z(1, halves[1], z1_halves[1])
-        for b in range(N_TILES // 2):
-            second_stage(1, 1, b)
-        finish(0, 1)
+        for q in (0, 1):
+            make_z(nc.vector, 1, quarters[q], z_quarters[q])
+        for q in (0, 1):
+            quantise_z(1, quarters[q], z_quarters[q][:])
+        second_product(0, 0)
+        second_product(1, 0)
+        second_product(0, 1)
+        for q in (2, 3):
+            make_z(nc.vector, 1, quarters[q], z_quarters[q])
+            finish(0, q - 2)
+        for q in (2, 3):
+            quantise_z(1, quarters[q], z_quarters[q][:])
+        second_product(1, 1)
         finish(0, 2)
-        for b in range(N_TILES // 2):
-            finish(1, b)
+        finish(1, 0)
+        finish(1, 1)
+        finish(1, 2, 0, 1)
+        finish(1, 2, 1, 2)

import math
from contextlib import ExitStack

import concourse.mybir as mybir

K, T, S, PAIRS, H, N = 512, 2048, 1024, 512, 1024, 768
FLOPS = 2 * K * H * S + 2 * H * N * PAIRS

F32 = mybir.dt.float32
BF16 = mybir.dt.bfloat16
I32 = mybir.dt.int32
U32 = mybir.dt.uint32
U16 = mybir.dt.uint16
U8 = mybir.dt.uint8
FP8X4 = mybir.dt.float8_e4m3fn_x4
FP4X4 = mybir.dt.float4_e2m1fn_x4
ACT = mybir.ActivationFunctionType
ALU = mybir.AluOpType

P = 128
PACK = 4
K_PASS = P * PACK
BANK = 512
GROUP = 16
QUADRANT = 32
SCALE_ROWS = 4
STRADDLE = GROUP - SCALE_ROWS // 2
PASSES = H // K_PASS
SLICES = H // P
LAST = SLICES - 1
N_TILES = N // P
W1_PIECE = 256
HALF = PAIRS // 2
QUARTER = PAIRS // 4
SHARES = (slice(0, 128), slice(128, 320), slice(320, 512))


def tile_list_audit_schedule_priorities_kernel(
    tc, tab_words, tab_scales, offs, w1, pos1, pos2, lift, w4_words, w4_scales, base, out
):
    nc = tc.nc
    with ExitStack() as ctx:
        keep = ctx.enter_context(tc.tile_pool(name="keep", bufs=1))
        ring = ctx.enter_context(tc.tile_pool(name="ring", bufs=1))
        psum = ctx.enter_context(tc.psum_pool(name="psum", bufs=8))

        def held(shape, dtype, name):
            return keep.tile(shape, dtype, name=name, align_bytes=64)

        offs_t = keep.tile([P, S // GROUP], U16, name="offs_t")
        pos1_t = keep.tile([P, PAIRS // GROUP], U16, name="pos1_t")
        pos2_t = keep.tile([P, PAIRS // GROUP], U16, name="pos2_t")
        tab_w = held([P, T], I32, "tab_w")
        tab_s = held([P, T], U8, "tab_s")
        v_w = [held([P, BANK], U32, "v_w%d" % i) for i in range(2)]
        v_s_picked = held([P, S], U8, "v_s_picked")
        v_s = held([P, S], U8, "v_s")
        zero = keep.tile([P, 1], F32, name="zero")
        no_bias = keep.tile([P, 1], F32, name="no_bias")
        half_lift = keep.tile([P, SLICES], F32, name="half_lift")

        nc.gpsimd.memset(tab_s[:].bitcast(I32), 0)
        nc.gpsimd.memset(zero[:], 0.0)
        nc.gpsimd.memset(v_s[:].bitcast(I32), 0)
        nc.scalar.activation(no_bias[:], zero[:], ACT.Silu)

        nc.sync.dma_start(offs_t[:], offs)
        for d in range(P // QUADRANT):
            r0 = QUADRANT * d + STRADDLE
            rows = tab_scales[0, SCALE_ROWS * d : SCALE_ROWS * (d + 1), :]
            nc.sync.dma_start(tab_s[r0 : r0 + SCALE_ROWS, :].bitcast(I32), rows.bitcast(I32))
        w1_rows = w1.rearrange("(p j) c -> p j c", j=PACK)
        w1_raw = {}

        def load_w1(piece, name):
            w1_raw[piece] = held([P, PACK, W1_PIECE], F32, name)
            nc.sync.dma_start(w1_raw[piece][:], w1_rows[:, :, W1_PIECE * piece : W1_PIECE * (piece + 1)])

        load_w1(0, "w1_raw0")
        nc.sync.dma_start(tab_w[:], tab_words[0].rearrange("p t i -> p (t i)").bitcast(I32))
        load_w1(1, "w1_raw1")
        load_w1(2, "w1_raw2")
        nc.sync.dma_start(pos2_t[:], pos2)
        nc.sync.dma_start(pos1_t[:], pos1)

        nc.vector.tensor_copy(v_s_picked[:], tab_s[:].indirect(offs_t[:]))
        for r0, count in ((0, SCALE_ROWS), (QUADRANT, 2 * QUADRANT), (3 * QUADRANT, SCALE_ROWS)):
            nc.sync.dma_start(
                v_s[r0 : r0 + count, :].bitcast(I32), v_s_picked[r0 + STRADDLE : r0 + STRADDLE + count, :].bitcast(I32)
            )
        load_w1(3, "tab_s")

        w1_w = [held([P, K_PASS], U32, "w1_w%d" % a) for a in range(PASSES)]
        w1_s = [held([P, K_PASS], U8, "w1_s%d" % a) for a in range(PASSES)]

        def deal_w1(copy, dealt, piece):
            m_count = W1_PIECE // PACK
            m0 = m_count * piece % P
            copy(
                dealt[:, :, m0 : m0 + m_count, :].rearrange("p t m j -> p m j t"),
                w1_raw[piece][:].rearrange("p j (m t) -> p m j t", t=PACK),
            )

        def quantise_w1(a, dealt, t0, t1):
            cols = slice(P * t0, P * t1)
            nc.vector.quantize_mx(
                out=w1_w[a][:, cols].bitcast(FP8X4),
                scales=w1_s[a][:, cols],
                in_=dealt[:, t0:t1, :, :].rearrange("p t m j -> p (t m j)"),
            )

        dealt = held([P, PACK, P, PACK], BF16, "dealt")
        for piece in (0, 1):
            deal_w1(nc.scalar.copy, dealt, piece)
        for i in range(2):
            entries = offs_t[:, BANK // GROUP * i : BANK // GROUP * (i + 1)]
            nc.vector.tensor_copy(v_w[i][:], tab_w[:].bitcast(U32).indirect(entries))
        quantise_w1(0, dealt, 0, 2)
        quantise_w1(0, dealt, 2, 4)
        dealt = held([P, PACK, P, PACK], BF16, "dealt")
        for piece in (2, 3):
            deal_w1(nc.vector.tensor_copy, dealt, piece)
        quantise_w1(1, dealt, 0, 4)

        lift_t = held([P, PASSES, PACK], F32, "v_s_picked")
        w4_s = held([P, PASSES, N], U8, "w1_raw0")
        w4_w = held([P, PASSES, 2 * N], U8, "w1_raw1")
        base_t = held([P, N_TILES, PAIRS], F32, "tab_w")
        nc.gpsimd.memset(w4_s[:].rearrange("p a c -> p (a c)").bitcast(I32), 0)
        nc.sync.dma_start(lift_t[:], lift.rearrange("(a p t) -> p a t", p=P, t=PACK))
        nc.gpsimd.tensor_scalar(half_lift[:], lift_t[:].rearrange("p a t -> p (a t)"), 0.5, 0.0, ALU.mult, ALU.add)
        for d in range(P // QUADRANT):
            rows = w4_scales[:, SCALE_ROWS * d : SCALE_ROWS * (d + 1), :].rearrange("a q c -> q a c")
            nc.sync.dma_start(w4_s[QUADRANT * d : QUADRANT * d + SCALE_ROWS, :, :].bitcast(I32), rows.bitcast(I32))
        nc.sync.dma_start(w4_w[:].bitcast(I32), w4_words.rearrange("a p c -> p a c").bitcast(I32))
        nc.sync.dma_start(base_t[:], base.rearrange("(nt p) m -> p nt m", p=P))

        last_year = [keep.tile([P, PACK, PAIRS], F32, name="last_year%d" % a) for a in range(PASSES)]
        gate = [keep.tile([P, PACK, PAIRS], F32, name="gate%d" % a) for a in range(PASSES)]
        first_sines = keep.tile([P, 2, BANK], F32, name="first_sines")
        z_s = [held([P, PAIRS], U8, "z_s%d" % a) for a in range(PASSES)]
        a_banks, squares, h_tiles, z_w, z_shares = {}, {}, {}, {}, {}
        halves = [slice(HALF * i, HALF * (i + 1)) for i in range(2)]
        quarters = [slice(QUARTER * i, QUARTER * (i + 1)) for i in range(4)]

        def sines(s, i):
            if s <= 1:
                return first_sines[:, i, :]
            a, t = divmod(s - 1, PACK)
            return (last_year, gate)[i][a][:, t, :]

        def first_product(s):
            a, t = divmod(s, PACK)
            cols = slice(P * t, P * (t + 1))
            for i in range(2):
                a_banks[s, i] = psum.tile([P, BANK], F32, name="bank")
                nc.tensor.matmul_mx(
                    out=a_banks[s, i][:],
                    lhsT=w1_w[a][:, cols].bitcast(FP8X4),
                    lhsT_scale=w1_s[a][:, cols],
                    rhs=v_w[i][:].bitcast(FP8X4),
                    rhs_scale=v_s[:, BANK * i : BANK * (i + 1)],
                    start=True,
                    stop=True,
                )
            for i in range(2):
                nc.scalar.activation(sines(s, i), a_banks[s, i][:], ACT.Sin, bias=no_bias[:], scale=0.5)
            for i in range(2):
                squares[s, i] = ring.tile([P, BANK], F32, name="square", bufs=4)
                nc.scalar.activation(squares[s, i][:], sines(s, i), ACT.Square, scale=math.sqrt(2.0))
            h_tiles[s] = held([P, S], F32, "h%d" % s)

        def features(s, i):
            nc.vector.scalar_tensor_tensor(
                h_tiles[s][:, BANK * i : BANK * (i + 1)], a_banks[s, i][:], 1.0, squares[s, i][:], ALU.add, ALU.subtract
            )

        def pick_last_year(s):
            a, t = divmod(s, PACK)
            nc.vector.tensor_copy(last_year[a][:, t, :], h_tiles[s][:].indirect(pos2_t[:]))

        def pick_difference(s, cols):
            a, t = divmod(s, PACK)
            this_year = h_tiles[s][:].indirect(pos1_t[:, cols.start // GROUP : cols.stop // GROUP])
            nc.vector.tensor_tensor(gate[a][:, t, cols], this_year, last_year[a][:, t, cols], ALU.subtract)

        def make_gate(s, *pieces):
            a, t = divmod(s, PACK)
            factor = half_lift[:, s : s + 1]
            for cols in pieces:
                nc.scalar.activation(gate[a][:, t, cols], gate[a][:, t, cols], ACT.Tanh, scale=0.5)
            for cols in pieces:
                nc.scalar.activation(gate[a][:, t, cols], gate[a][:, t, cols], ACT.Identity, bias=factor, scale=factor)

        def make_z(engine, a, cols, z):
            engine.tensor_tensor(
                z[:].rearrange("p (c i t) -> p c t i", i=4, t=PACK),
                gate[a][:, :, cols].rearrange("p t (c i) -> p c t i", i=4),
                last_year[a][:, :, cols].rearrange("p t (c i) -> p c t i", i=4),
                ALU.mult,
            )

        def quantise_z(a, cols, z):
            nc.vector.quantize_mx(out=z_w[a][:, cols].bitcast(FP8X4), scales=z_s[a][:, cols], in_=z)

        def make_share(q, name):
            z_shares[q] = held([P, PACK * (SHARES[q].stop - SHARES[q].start)], BF16, name)
            make_z(nc.gpsimd, 0, SHARES[q], z_shares[q])

        def quantise_share(q, start, stop):
            c0 = SHARES[q].start
            quantise_z(0, slice(start, stop), z_shares[q][:, PACK * (start - c0) : PACK * (stop - c0)])

        every_pair = slice(0, PAIRS)
        first_product(0)
        features(0, 0)
        features(0, 1)
        pick_last_year(0)
        pick_difference(0, every_pair)
        first_product(1)
        features(1, 0)
        features(1, 1)
        for s in range(1, LAST):
            first_product(s + 1)
            features(s + 1, 0)
            pick_last_year(s)
            features(s + 1, 1)
            pick_difference(s, every_pair)
            if s - 1 == PACK - 1:
                make_gate(s - 1, SHARES[0])
                make_share(0, "z_share0")
                make_gate(s - 1, slice(SHARES[0].stop, PAIRS))
            else:
                make_gate(s - 1, every_pair)
            if s in (PACK, PACK + 1):
                make_share(s - PACK + 1, "h%d" % s)
        make_gate(LAST - 1, every_pair)

        z_w[0] = held([P, PAIRS], U32, "h%d" % (LAST - 1))
        z_w[1] = held([P, PAIRS], U32, "z_w1")
        z_quarters = [held([P, PACK * QUARTER], BF16, "z_quarter%d" % q) for q in range(4)]
        pick_last_year(LAST)
        quantise_share(0, 0, 128)
        quantise_share(1, 128, 256)
        for cols in halves:
            pick_difference(LAST, cols)
        make_gate(LAST, quarters[0], quarters[1])
        make_gate(LAST, quarters[2], quarters[3])
        quantise_share(1, 256, 320)
        quantise_share(2, 320, 384)
        quantise_share(2, 384, 512)

        banks = range(N_TILES // 2)
        y_banks = {(i, b): psum.tile([P, 2, HALF], F32, name="bank") for i in range(2) for b in banks}

        def second_product(a, i):
            for b in banks:
                for c in range(2):
                    cols = quarters[2 * i + c]
                    for u in range(2):
                        nt = 2 * b + u
                        nc.tensor.matmul_mx(
                            out=y_banks[i, b][:, u, QUARTER * c : QUARTER * (c + 1)],
                            lhsT=w4_w[:, a, 2 * P * nt : 2 * P * (nt + 1)].bitcast(FP4X4),
                            lhsT_scale=w4_s[:, a, P * nt : P * (nt + 1)],
                            rhs=z_w[a][:, cols].bitcast(FP8X4),
                            rhs_scale=z_s[a][:, cols],
                            start=(a, c, u) == (0, 0, 0),
                            stop=(a, c, u) == (PASSES - 1, 1, 1),
                        )

        out_rows = out.rearrange("(nt p) m -> p nt m", p=P)

        def finish(i, b, u0=0, u1=2):
            tiles = slice(2 * b + u0, 2 * b + u1)
            result = held([P, u1 - u0, HALF], F32, "result%d_%d" % (i, tiles.start))
            nc.vector.tensor_tensor(result[:], y_banks[i, b][:, u0:u1, :], base_t[:, tiles, halves[i]], ALU.add)
            nc.sync.dma_start(out_rows[:, tiles, halves[i]], result[:])

        for q in (0, 1):
            make_z(nc.vector, 1, quarters[q], z_quarters[q])
        for q in (0, 1):
            quantise_z(1, quarters[q], z_quarters[q][:])
        second_product(0, 0)
        second_product(1, 0)
        second_product(0, 1)
        for q in (2, 3):
            make_z(nc.vector, 1, quarters[q], z_quarters[q])
            finish(0, q - 2)
        for q in (2, 3):
            quantise_z(1, quarters[q], z_quarters[q][:])
        second_product(1, 1)
        finish(0, 2)
        finish(1, 0)
        finish(1, 1)
        finish(1, 2, 0, 1)
        finish(1, 2, 1, 2)
